import numpy as np
import ml_dtypes


def mxq(x, axis, fmt="e4m3"):
    dtype, down = {"e4m3": (ml_dtypes.float8_e4m3fn, 7), "e5m2": (ml_dtypes.float8_e5m2, 14)}[fmt]
    v = np.moveaxis(np.asarray(x, np.float32).astype(ml_dtypes.bfloat16).astype(np.float64), axis, -1)
    blocks = v.reshape(v.shape[:-1] + (-1, 32))
    amax = np.abs(blocks).max(-1, keepdims=True)
    byte = np.maximum(np.where(amax > 0, np.frexp(amax)[1] - 1 + 127, 0) - down, 1)
    scale = np.exp2(byte - 127.0)
    codes = (blocks / scale).astype(np.float32).astype(dtype).astype(np.float64)
    return np.moveaxis((codes * scale).reshape(v.shape), -1, axis)


WIDE = False


def mx_kscale(k):
    if not WIDE:
        return np.ones(k)
    levels = np.array([30, -30])
    if k % 512:
        return np.exp2(np.random.permutation(np.resize(levels, k // 32))).repeat(32)
    a = np.empty((k // 512, 16))
    for p in range(k // 512):
        a[p, :8] = np.random.permutation(np.resize(levels, 8))
        for g in range(8):
            far = levels[np.abs(levels - a[p, g]) >= 10]
            a[p, g + 8] = far[np.random.randint(len(far))]
    return np.exp2(a.ravel()).repeat(32)


def f64(x):
    return np.asarray(x).astype(np.float64)


def striped(idx):
    return np.tile(np.asarray(idx).reshape(-1, 16).T, (8, 1)).astype(np.uint16)


def unstriped(offs):
    return offs[:16].T.reshape(-1).astype(np.int64)


E2M1 = np.array([0.0, 0.5, 1.0, 1.5, 2.0, 3.0, 4.0, 6.0, -0.0, -0.5, -1.0, -1.5, -2.0, -3.0, -4.0, -6.0])


def pack_weight(w, fmt):
    k, n = w.shape
    w = f64(np.asarray(w, np.float32).astype(ml_dtypes.bfloat16)).reshape(k // 32, 32, n)
    amax = np.abs(w).max(1)
    if fmt in ("e4m3", "e5m2"):
        byte = np.frexp(amax)[1] - 1 + 127 - (7 if fmt == "e4m3" else 14)
    else:
        mant, ex = np.frexp(amax / 6.0)
        byte = np.where(mant > 0.5, ex, ex - 1) + 127
    byte = np.clip(np.where(amax > 0, byte, 1), 1, 254)
    scaled = (w * np.exp2(127.0 - byte)[:, None, :]).reshape(k, n).astype(np.float32)
    by_word = np.ascontiguousarray(scaled.reshape(k // 512, 128, 4, n).transpose(0, 1, 3, 2))
    if fmt in ("e4m3", "e5m2"):
        words = by_word.astype(ml_dtypes.float8_e4m3fn if fmt == "e4m3" else ml_dtypes.float8_e5m2).view(np.uint8)
    else:
        c = by_word.astype(ml_dtypes.float4_e2m1fn).view(np.uint8) & 0xF
        words = (c[..., 0::2] | (c[..., 1::2] << 4)).reshape(k // 512, 128, 2 * n)
    return np.ascontiguousarray(words), np.ascontiguousarray(byte.astype(np.uint8).reshape(k // 512, 16, n))


def unpack_weight(words, scales, fmt):
    g, _, n = scales.shape
    words = np.ascontiguousarray(words).reshape(g, 128, n, -1)
    if fmt in ("e4m3", "e5m2"):
        vals = words.view(ml_dtypes.float8_e4m3fn if fmt == "e4m3" else ml_dtypes.float8_e5m2).astype(np.float64)
    else:
        nib = np.empty((g, 128, n, 4), np.uint8)
        nib[..., 0::2] = words & 0xF
        nib[..., 1::2] = words >> 4
        vals = E2M1[nib]
    vals = vals * np.repeat(np.exp2(scales.astype(np.float64) - 127.0), 8, axis=1)[..., None]
    return vals.transpose(0, 1, 3, 2).reshape(g * 512, n)


def bf(x):
    return np.asarray(x, np.float32).astype(ml_dtypes.bfloat16)


def planes(Y):
    r, m = Y.shape
    b = f64(bf(Y)).reshape(r // 32, 32, m)
    amax = np.abs(b).max(1)
    byte = np.clip(np.where(amax > 0, np.frexp(amax)[1] - 1 + 127 - 7, 1), 1, 254)
    codes = (b * np.exp2(127.0 - byte)[:, None, :]).reshape(r, m).astype(np.float32).astype(ml_dtypes.float8_e4m3fn).view(np.uint8)
    words = codes.reshape(r // 512, 128, 4, m).transpose(0, 1, 3, 2)
    return np.ascontiguousarray(words), np.ascontiguousarray(byte.astype(np.uint8).reshape(r // 512, 16, m))


K, T, J, S, R, L, N, C = 1024, 1024, 256, 512, 512, 512, 512, 1024


def setup_inputs():
    n = np.random.standard_normal
    idx = np.random.permutation(T)[:J]
    idx2 = np.random.permutation(S)[:J]
    idx3 = np.random.permutation(C)[:J]
    fk = mx_kscale(K)
    fr = mx_kscale(R)
    fl = mx_kscale(L)
    wp = pack_weight(n((K, R)) * 1 / np.sqrt(K) * fk[:, None] * fr, "e5m2")
    sxp = pack_weight(n((L, J)) / fl[:, None], "e5m2")
    wsp = pack_weight(n((L, R)) * 1 / np.sqrt(L) * fl[:, None] * fr, "e5m2")
    wbp = pack_weight(n((R, N)) * 1 / np.sqrt(R) / fr[:, None], "e2m1")
    return {
        "xa": (n((K, T))).astype(np.float32),
        "xb": (n((K, S))).astype(np.float32),
        "fk": (np.random.uniform(0.5, 2.0, (K, 1)) / fk[:, None]).astype(np.float32),
        "w_words": wp[0],
        "w_scales": wp[1],
        "sx_words": sxp[0],
        "sx_scales": sxp[1],
        "ws_words": wsp[0],
        "ws_scales": wsp[1],
        "wb_words": wbp[0],
        "wb_scales": wbp[1],
        "old": (1.0 * n((N, C))).astype(np.float32),
        "offs": striped(idx),
        "offs2": striped(idx2),
        "offs3": striped(idx3),
    }


def reference(xa, xb, fk, w_words, w_scales, sx_words, sx_scales, ws_words, ws_scales, wb_words, wb_scales, old, offs, offs2, offs3):
    idx = unstriped(offs)
    idx2 = unstriped(offs2)
    idx3 = unstriped(offs3)
    wu = unpack_weight(w_words, w_scales, "e5m2")
    sxu = unpack_weight(sx_words, sx_scales, "e5m2")
    wsu = unpack_weight(ws_words, ws_scales, "e5m2")
    wbu = unpack_weight(wb_words, wb_scales, "e2m1")
    u = f64(xa)[:, idx] * f64(xb)[:, idx2] * f64(fk)
    uq = mxq(u, 0, "e5m2")
    a = wu.T @ uq
    b2 = wsu.T @ sxu
    hid = np.maximum(a, b2)
    hidq = mxq(hid, 0, "e5m2")
    p = wbu.T @ hidq
    pp = np.zeros((N, C))
    pp[:, idx3] = p
    y = pp + 0.5 * f64(old)
    words, scales = planes(y)
    return y, words, scales

@@ -1,0 +1,248 @@
+from contextlib import ExitStack
+
+import concourse.mybir as mybir
+
+K, T, J, S, R, L, N, C = 1024, 1024, 256, 512, 512, 512, 512, 1024
+FLOPS = 2 * J * (K * R + L * R + R * N)
+
+F32 = mybir.dt.float32
+BF16 = mybir.dt.bfloat16
+I32 = mybir.dt.int32
+U32 = mybir.dt.uint32
+U16 = mybir.dt.uint16
+U8 = mybir.dt.uint8
+E5M2 = mybir.dt.float8_e5m2_x4
+E4M3 = mybir.dt.float8_e4m3fn_x4
+E2M1 = mybir.dt.float4_e2m1fn_x4
+ALU = mybir.AluOpType
+COPY = mybir.ActivationFunctionType.Copy
+
+P = 128
+PACK = 4
+PASSES = K // (P * PACK)
+HALF = J // 2
+LIST_COLS = J // 16
+CHUNK = 256
+
+
+def interleave(copy, dst, src):
+    copy(dst.rearrange("p (c i) t -> p c t i", i=4), src.rearrange("p t (c i) -> p c t i", i=4))
+
+
+def tile_list_entryproducts_rival_scattered_pl_kernel(
+    tc, xa, xb, fk, w_words, w_scales, sx_words, sx_scales, ws_words, ws_scales, wb_words, wb_scales,
+    old, offs, offs2, offs3, out_0, out_1, out_2,
+):
+    nc = tc.nc
+    with ExitStack() as ctx:
+        keep = ctx.enter_context(tc.tile_pool(name="keep", bufs=1))
+        psum = ctx.enter_context(tc.psum_pool(name="psum", bufs=1))
+
+        def sbuf(name, shape, dtype):
+            return keep.tile(shape, dtype, name=name, align_bytes=64)
+
+        list_a = keep.tile([P, LIST_COLS], U16, name="list_a")
+        list_b = keep.tile([P, LIST_COLS], U16, name="list_b")
+        list_c = keep.tile([P, LIST_COLS], U16, name="list_c")
+        factor = sbuf("factor", [P, PASSES, PACK], F32)
+
+        raw_scales = sbuf("raw_scales", [P, 4 * R], U8)
+        sx_sc = sbuf("sx_sc", [P, J], U8)
+        nc.vector.memset(raw_scales[:].bitcast(I32), 0)
+        nc.vector.memset(sx_sc[:].bitcast(I32), 0)
+        pages = [sbuf(f"page{t}", [P, C], F32) for t in range(PACK)]
+        for t in range(PACK):
+            nc.vector.memset(pages[t][:], 0.0)
+
+        def load_scales(dst, src, q):
+            nc.sync.dma_start(out=dst[32 * q : 32 * q + 4, :].bitcast(I32), in_=src[4 * q : 4 * q + 4, :].bitcast(I32))
+
+        xa_rows = xa.rearrange("(a p i) t -> a i p t", a=PASSES, i=PACK)
+        xb_rows = xb.rearrange("(a p u e) s -> a u p e s", a=PASSES, u=2, e=2)
+        xa_sb = [[sbuf(f"xa{a}_{i}", [P, T], F32) for i in range(PACK)] for a in range(PASSES)]
+        xb_sb = [[sbuf(f"xb{a}_{u}", [P, 2, S], F32) for u in range(2)] for a in range(PASSES)]
+        w_raw = [sbuf(f"w_raw{a}", [P, R], U32) for a in range(PASSES)]
+        ws_raw = sbuf("ws_raw", [P, R], U32)
+        sx_w = sbuf("sx_w", [P, J], U32)
+        wb_raw = sbuf("wb_raw", [P, 2 * N], U8)
+        old_sb = [sbuf(f"old{t}", [P, C], F32) for t in range(PACK)]
+
+        def load_words(dst, src):
+            nc.sync.dma_start(out=dst[:].bitcast(I32), in_=src.rearrange("p n t -> p (n t)").bitcast(I32))
+
+        def load_w_scales(q):
+            nc.sync.dma_start(
+                out=raw_scales[32 * q : 32 * q + 4, 0 : 2 * R].bitcast(I32).rearrange("r (a n) -> r a n", a=PASSES),
+                in_=w_scales.bitcast(I32)[:, 4 * q : 4 * q + 4, :].rearrange("a r n -> r a n"),
+            )
+
+        def load_xa(a, i):
+            nc.sync.dma_start(out=xa_sb[a][i][:], in_=xa_rows[a, i])
+
+        def load_xb(a, u):
+            nc.sync.dma_start(out=xb_sb[a][u][:], in_=xb_rows[a, u])
+
+        large = [
+            lambda: load_xb(0, 0), lambda: load_xa(0, 0), lambda: load_xa(0, 1), lambda: load_xb(0, 1),
+            lambda: load_xa(0, 2), lambda: load_xa(0, 3), lambda: load_words(ws_raw, ws_words[0]),
+            lambda: load_xb(1, 0), lambda: load_words(sx_w, sx_words[0]), lambda: load_xa(1, 0),
+            lambda: load_words(w_raw[0], w_words[0]), lambda: load_xa(1, 1), lambda: load_words(w_raw[1], w_words[1]),
+            lambda: load_xb(1, 1),
+            lambda: nc.sync.dma_start(out=wb_raw[:].bitcast(I32), in_=wb_words[0].bitcast(I32)),
+            lambda: load_xa(1, 2), lambda: load_xa(1, 3),
+        ]
+        small = [
+            lambda: nc.sync.dma_start(list_b[:], offs2),
+            lambda: nc.sync.dma_start(out=factor[:], in_=fk.rearrange("(a p i) o -> p a (i o)", a=PASSES, i=PACK)),
+            lambda: nc.sync.dma_start(list_a[:], offs),
+        ]
+        small = small + [lambda q=q: load_scales(raw_scales[:, 2 * R : 3 * R], ws_scales[0], q) for q in range(4)]
+        small = small + [lambda q=q: load_scales(sx_sc[:], sx_scales[0], q) for q in range(4)]
+        small = small + [lambda q=q: load_w_scales(q) for q in range(4)]
+        small = small + [lambda q=q: load_scales(raw_scales[:, 3 * R : 4 * R], wb_scales[0], q) for q in range(4)]
+        taken = 0
+        for n, load in enumerate(large):
+            load()
+            upto = min(len(small), (n + 1) * len(small) // (len(large) - 2) + 1)
+            for load_small in small[taken:upto]:
+                load_small()
+            taken = upto
+        nc.sync.dma_start(list_c[:], offs3)
+        old_rows = old.rearrange("(p t) c -> t p c", t=PACK)
+        for t in range(PACK):
+            nc.sync.dma_start(out=old_sb[t][:], in_=old_rows[t])
+
+        def deal(name, raw, dtype):
+            dealt = sbuf(name, [P, PACK, P], dtype)
+            nc.vector.tensor_copy(dealt[:], raw.rearrange("p (m t) -> p t m", t=PACK))
+            return dealt
+
+        picked_b = sbuf("picked_b", [P, PASSES * PACK, J], F32)
+        scaled_b = sbuf("scaled_b", [P, PASSES * PACK, J], F32)
+        u_planes = [sbuf(f"u_planes{a}", [P, PACK, J], F32) for a in range(PASSES)]
+
+        def pick_b(a, i):
+            n = a * PACK + i
+            nc.scalar.activation(picked_b[:, n, :], xb_sb[a][i // 2][:, i % 2, :].indirect(list_b[:]), COPY)
+            nc.scalar.activation(scaled_b[:, n, :], picked_b[:, n, :], COPY, scale=factor[:, a, i : i + 1])
+
+        def pick_a(a, i, cols, list_cols):
+            nc.vector.tensor_tensor(
+                u_planes[a][:, i, cols], xa_sb[a][i][:].indirect(list_a[:, list_cols]),
+                scaled_b[:, a * PACK + i, cols], ALU.mult,
+            )
+
+        halves = [slice(h * HALF, (h + 1) * HALF) for h in range(2)]
+        list_halves = [slice(h * LIST_COLS // 2, (h + 1) * LIST_COLS // 2) for h in range(2)]
+        whole, list_whole = slice(0, J), slice(0, LIST_COLS)
+
+        for i in range(PACK):
+            pick_b(0, i)
+            pick_a(0, i, whole, list_whole)
+        ws_d = deal("ws_d", ws_raw[:], U32)
+        ws_sd = deal("ws_sd", raw_scales[:, 2 * R : 3 * R], U8)
+        b2_sb = []
+        for h in range(2):
+            bank = psum.tile([P, PACK, HALF], F32, name=f"b2_bank{h}")
+            for t in range(PACK):
+                nc.tensor.matmul_mx(
+                    out=bank[:, t, :], lhsT=ws_d[:, t, :].bitcast(E5M2), lhsT_scale=ws_sd[:, t, :],
+                    rhs=sx_w[:, halves[h]].bitcast(E5M2), rhs_scale=sx_sc[:, halves[h]], start=True, stop=True,
+                )
+            held = sbuf(f"b2_sb{h}", [P, HALF, PACK], F32)
+            nc.scalar.copy(held[:], bank[:].rearrange("p t j -> p j t"))
+            b2_sb.append(held)
+
+        u_bf = [[sbuf(f"u_bf{a}_{h}", [P, HALF, PACK], BF16) for h in range(2)] for a in range(PASSES)]
+        u_codes = [[sbuf(f"u_codes{a}_{h}", [P, HALF], U32) for h in range(2)] for a in range(PASSES)]
+        u_sc = [[sbuf(f"u_sc{a}_{h}", [P, HALF], U8) for h in range(2)] for a in range(PASSES)]
+        a_banks = [psum.tile([P, PACK, HALF], F32, name=f"a_bank{h}") for h in range(2)]
+        w_d, w_sd = [], []
+
+        def first_product(a):
+            for h in range(2):
+                interleave(nc.vector.tensor_copy, u_bf[a][h][:], u_planes[a][:, :, halves[h]])
+            for h in range(2):
+                nc.vector.quantize_mx(
+                    out=u_codes[a][h][:].bitcast(E5M2), scales=u_sc[a][h][:],
+                    in_=u_bf[a][h][:].rearrange("p j t -> p (j t)"),
+                )
+            for h in range(2):
+                for t in range(PACK):
+                    nc.tensor.matmul_mx(
+                        out=a_banks[h][:, t, :], lhsT=w_d[a][:, t, :].bitcast(E5M2), lhsT_scale=w_sd[a][:, t, :],
+                        rhs=u_codes[a][h][:].bitcast(E5M2), rhs_scale=u_sc[a][h][:],
+                        start=(a == 0 and t == 0), stop=(a == PASSES - 1 and t == PACK - 1),
+                    )
+
+        w_d.append(deal("w_d0", w_raw[0][:], U32))
+        w_sd.append(deal("w_sd0", raw_scales[:, 0:R], U8))
+        first_product(0)
+
+        for i in range(PACK - 1):
+            pick_b(1, i)
+            pick_a(1, i, whole, list_whole)
+        w_d.append(deal("w_d1", w_raw[1][:], U32))
+        w_sd.append(deal("w_sd1", raw_scales[:, R : 2 * R], U8))
+        wb_d = deal("wb_d", wb_raw[:].bitcast(U16), U16)
+        wb_sd = deal("wb_sd", raw_scales[:, 3 * R : 4 * R], U8)
+        pick_b(1, PACK - 1)
+        for h in range(2):
+            pick_a(1, PACK - 1, halves[h], list_halves[h])
+        first_product(1)
+
+        hid_bf = [sbuf(f"hid_bf{h}", [P, HALF, PACK], BF16) for h in range(2)]
+        hid_codes = [sbuf(f"hid_codes{h}", [P, HALF], U32) for h in range(2)]
+        hid_sc = [sbuf(f"hid_sc{h}", [P, HALF], U8) for h in range(2)]
+        p_banks = [psum.tile([P, PACK, HALF], F32, name=f"p_bank{h}") for h in range(2)]
+        p_sb = sbuf("p_sb", [P, PACK, J], F32)
+        for h in range(2):
+            nc.vector.tensor_tensor(hid_bf[h][:], a_banks[h][:].rearrange("p t j -> p j t"), b2_sb[h][:], ALU.max)
+        for h in range(2):
+            nc.vector.quantize_mx(
+                out=hid_codes[h][:].bitcast(E5M2), scales=hid_sc[h][:],
+                in_=hid_bf[h][:].rearrange("p j t -> p (j t)"),
+            )
+            for t in range(PACK):
+                nc.tensor.matmul_mx(
+                    out=p_banks[h][:, t, :], lhsT=wb_d[:, t, :].bitcast(E2M1), lhsT_scale=wb_sd[:, t, :],
+                    rhs=hid_codes[h][:].bitcast(E5M2), rhs_scale=hid_sc[h][:], start=True, stop=True,
+                )
+        nc.scalar.copy(p_sb[:, :, halves[0]], p_banks[0][:])
+        nc.vector.tensor_copy(p_sb[:, :, halves[1]], p_banks[1][:])
+
+        y = sbuf("y", [P, PACK, C], F32)
+        out_rows = out_0.rearrange("(p t) c -> t p c", t=PACK)
+
+        def add_old(t, cols):
+            nc.vector.scalar_tensor_tensor(y[:, t, cols], old_sb[t][:, cols], 0.5, pages[t][:, cols], ALU.mult, ALU.add)
+
+        for h in range(2):
+            nc.scalar.activation(pages[0][:].indirect(list_c[:, list_halves[h]]), p_sb[:, 0, halves[h]], COPY)
+        nc.vector.tensor_copy(pages[1][:].indirect(list_c[:]), p_sb[:, 1, :])
+        for t in (2, 3):
+            nc.scalar.activation(pages[t][:].indirect(list_c[:]), p_sb[:, t, :], COPY)
+        for t in range(PACK - 1):
+            add_old(t, slice(0, C))
+            nc.sync.dma_start(out=out_rows[t], in_=y[:, t, :])
+        chunks = [slice(c0, c0 + CHUNK) for c0 in range(0, C, CHUNK)]
+        for cols in chunks:
+            add_old(PACK - 1, cols)
+        nc.sync.dma_start(out=out_rows[PACK - 1], in_=y[:, PACK - 1, :])
+
+        y_codes = sbuf("y_codes", [P, C], U32)
+        y_sc = sbuf("y_sc", [P, C], U8)
+        y_bf = [sbuf(f"y_bf{n}", [P, CHUNK, PACK], BF16) for n in range(len(chunks))]
+        words_out = out_1[0].rearrange("p c t -> p (c t)").bitcast(I32)
+        rounders = [nc.scalar.copy, nc.vector.tensor_copy, nc.vector.tensor_copy, nc.scalar.copy]
+        for n, cols in enumerate(chunks):
+            interleave(rounders[n], y_bf[n][:], y[:, :, cols])
+        for n, cols in enumerate(chunks):
+            nc.vector.quantize_mx(
+                out=y_codes[:, cols].bitcast(E4M3), scales=y_sc[:, cols],
+                in_=y_bf[n][:].rearrange("p c t -> p (c t)"),
+            )
+            nc.sync.dma_start(out=words_out[:, cols], in_=y_codes[:, cols].bitcast(I32))
+        for q in range(4):
+            queue = nc.sync if q % 2 == 0 else nc.scalar
+            queue.dma_start(out=out_2[0, 4 * q : 4 * q + 4, :].bitcast(I32), in_=y_sc[32 * q : 32 * q + 4, :].bitcast(I32))

@@ -23,6 +23,7 @@ PASSES = K // (P * PACK)
 HALF = J // 2
 LIST_COLS = J // 16
 CHUNK = 256
+SCALE_COLS = 4 * R + J
 
 
 def interleave(copy, dst, src):
@@ -46,22 +47,31 @@ def tile_list_entryproducts_rival_scattered_pl_kernel(
         list_c = keep.tile([P, LIST_COLS], U16, name="list_c")
         factor = sbuf("factor", [P, PASSES, PACK], F32)
 
-        raw_scales = sbuf("raw_scales", [P, 4 * R], U8)
-        sx_sc = sbuf("sx_sc", [P, J], U8)
-        nc.vector.memset(raw_scales[:].bitcast(I32), 0)
-        nc.vector.memset(sx_sc[:].bitcast(I32), 0)
+        staged = sbuf("staged", [P, 4, SCALE_COLS // 4], I32)
+        scales = sbuf("scales", [P, SCALE_COLS], U8)
+        scale_words = scales[:].bitcast(I32)
+        nc.vector.memset(scale_words, 0)
         pages = [sbuf(f"page{t}", [P, C], F32) for t in range(PACK)]
         for t in range(PACK):
             nc.vector.memset(pages[t][:], 0.0)
 
-        def load_scales(dst, src, q):
-            nc.sync.dma_start(out=dst[32 * q : 32 * q + 4, :].bitcast(I32), in_=src[4 * q : 4 * q + 4, :].bitcast(I32))
+        def load_scales(start, src):
+            width = src.shape[1] // 4
+            nc.sync.dma_start(
+                out=staged[0:P:32, :, start // 4 : start // 4 + width],
+                in_=src.bitcast(I32).rearrange("(q r) n -> q r n", r=4),
+            )
 
+        def spread_scales(r):
+            nc.sync.dma_start(out=scale_words[r:P:32, :], in_=staged[0:P:32, r, :])
+
+        xa_pairs = xa.rearrange("(a p u e) t -> a u p e t", a=PASSES, u=2, e=2)
         xa_rows = xa.rearrange("(a p i) t -> a i p t", a=PASSES, i=PACK)
-        xb_rows = xb.rearrange("(a p u e) s -> a u p e s", a=PASSES, u=2, e=2)
-        xa_sb = [[sbuf(f"xa{a}_{i}", [P, T], F32) for i in range(PACK)] for a in range(PASSES)]
-        xb_sb = [[sbuf(f"xb{a}_{u}", [P, 2, S], F32) for u in range(2)] for a in range(PASSES)]
-        w_raw = [sbuf(f"w_raw{a}", [P, R], U32) for a in range(PASSES)]
+        xb_rows = xb.rearrange("(a p i) s -> a p i s", a=PASSES, i=PACK)
+        xa_first = [sbuf(f"xa0_{u}", [P, 2, T], F32) for u in range(2)]
+        xa_last = [sbuf(f"xa1_{i}", [P, T], F32) for i in range(PACK)]
+        xb_sb = [sbuf(f"xb{a}", [P, PACK, S], F32) for a in range(PASSES)]
+        w_raw = sbuf("w_raw", [P, PASSES, R], U32)
         ws_raw = sbuf("ws_raw", [P, R], U32)
         sx_w = sbuf("sx_w", [P, J], U32)
         wb_raw = sbuf("wb_raw", [P, 2 * N], U8)
@@ -70,43 +80,26 @@ def tile_list_entryproducts_rival_scattered_pl_kernel(
         def load_words(dst, src):
             nc.sync.dma_start(out=dst[:].bitcast(I32), in_=src.rearrange("p n t -> p (n t)").bitcast(I32))
 
-        def load_w_scales(q):
-            nc.sync.dma_start(
-                out=raw_scales[32 * q : 32 * q + 4, 0 : 2 * R].bitcast(I32).rearrange("r (a n) -> r a n", a=PASSES),
-                in_=w_scales.bitcast(I32)[:, 4 * q : 4 * q + 4, :].rearrange("a r n -> r a n"),
-            )
-
-        def load_xa(a, i):
-            nc.sync.dma_start(out=xa_sb[a][i][:], in_=xa_rows[a, i])
-
-        def load_xb(a, u):
-            nc.sync.dma_start(out=xb_sb[a][u][:], in_=xb_rows[a, u])
-
-        large = [
-            lambda: load_xb(0, 0), lambda: load_xa(0, 0), lambda: load_xa(0, 1), lambda: load_xb(0, 1),
-            lambda: load_xa(0, 2), lambda: load_xa(0, 3), lambda: load_words(ws_raw, ws_words[0]),
-            lambda: load_xb(1, 0), lambda: load_words(sx_w, sx_words[0]), lambda: load_xa(1, 0),
-            lambda: load_words(w_raw[0], w_words[0]), lambda: load_xa(1, 1), lambda: load_words(w_raw[1], w_words[1]),
-            lambda: load_xb(1, 1),
-            lambda: nc.sync.dma_start(out=wb_raw[:].bitcast(I32), in_=wb_words[0].bitcast(I32)),
-            lambda: load_xa(1, 2), lambda: load_xa(1, 3),
-        ]
-        small = [
-            lambda: nc.sync.dma_start(list_b[:], offs2),
-            lambda: nc.sync.dma_start(out=factor[:], in_=fk.rearrange("(a p i) o -> p a (i o)", a=PASSES, i=PACK)),
-            lambda: nc.sync.dma_start(list_a[:], offs),
-        ]
-        small = small + [lambda q=q: load_scales(raw_scales[:, 2 * R : 3 * R], ws_scales[0], q) for q in range(4)]
-        small = small + [lambda q=q: load_scales(sx_sc[:], sx_scales[0], q) for q in range(4)]
-        small = small + [lambda q=q: load_w_scales(q) for q in range(4)]
-        small = small + [lambda q=q: load_scales(raw_scales[:, 3 * R : 4 * R], wb_scales[0], q) for q in range(4)]
-        taken = 0
-        for n, load in enumerate(large):
-            load()
-            upto = min(len(small), (n + 1) * len(small) // (len(large) - 2) + 1)
-            for load_small in small[taken:upto]:
-                load_small()
-            taken = upto
+        nc.sync.dma_start(out=xb_sb[0][:], in_=xb_rows[0])
+        load_scales(0, w_scales[0])
+        load_scales(R, w_scales[1])
+        load_scales(2 * R, ws_scales[0])
+        load_scales(3 * R, wb_scales[0])
+        load_scales(4 * R, sx_scales[0])
+        nc.sync.dma_start(list_b[:], offs2)
+        nc.sync.dma_start(out=xa_first[0][:], in_=xa_pairs[0, 0])
+        nc.sync.dma_start(list_a[:], offs)
+        nc.sync.dma_start(out=factor[:], in_=fk.rearrange("(a p i) o -> p a (i o)", a=PASSES, i=PACK))
+        for r in range(4):
+            spread_scales(r)
+        nc.sync.dma_start(out=xa_first[1][:], in_=xa_pairs[0, 1])
+        nc.sync.dma_start(out=xb_sb[1][:], in_=xb_rows[1])
+        nc.sync.dma_start(out=w_raw[:].bitcast(I32), in_=w_words.rearrange("a p n t -> p a (n t)").bitcast(I32))
+        load_words(ws_raw, ws_words[0])
+        nc.sync.dma_start(out=wb_raw[:].bitcast(I32), in_=wb_words[0].bitcast(I32))
+        for i in range(PACK):
+            nc.sync.dma_start(out=xa_last[i][:], in_=xa_rows[1, i])
+        load_words(sx_w, sx_words[0])
         nc.sync.dma_start(list_c[:], offs3)
         old_rows = old.rearrange("(p t) c -> t p c", t=PACK)
         for t in range(PACK):
@@ -114,22 +107,29 @@ def tile_list_entryproducts_rival_scattered_pl_kernel(
 
         def deal(name, raw, dtype):
             dealt = sbuf(name, [P, PACK, P], dtype)
-            nc.vector.tensor_copy(dealt[:], raw.rearrange("p (m t) -> p t m", t=PACK))
+            nc.vector.tensor_copy(dealt[:].rearrange("p t m -> p m t"), raw.rearrange("p (m t) -> p m t", t=PACK))
             return dealt
 
         picked_b = sbuf("picked_b", [P, PASSES * PACK, J], F32)
-        scaled_b = sbuf("scaled_b", [P, PASSES * PACK, J], F32)
+        picked_a = sbuf("picked_a", [P, PACK, J], F32)
+        scaled_b = sbuf("scaled_b", [P, PACK, J], F32)
         u_planes = [sbuf(f"u_planes{a}", [P, PACK, J], F32) for a in range(PASSES)]
 
         def pick_b(a, i):
-            n = a * PACK + i
-            nc.scalar.activation(picked_b[:, n, :], xb_sb[a][i // 2][:, i % 2, :].indirect(list_b[:]), COPY)
-            nc.scalar.activation(scaled_b[:, n, :], picked_b[:, n, :], COPY, scale=factor[:, a, i : i + 1])
+            nc.scalar.activation(picked_b[:, a * PACK + i, :], xb_sb[a][:, i, :].indirect(list_b[:]), COPY)
 
-        def pick_a(a, i, cols, list_cols):
+        def first_plane(i):
+            nc.scalar.activation(picked_a[:, i, :], xa_first[i // 2][:, i % 2, :].indirect(list_a[:]), COPY)
+            nc.vector.scalar_tensor_tensor(
+                u_planes[0][:, i, :], picked_a[:, i, :], factor[:, 0, i : i + 1], picked_b[:, i, :], ALU.mult, ALU.mult
+            )
+
+        def scale_b(i):
+            nc.scalar.activation(scaled_b[:, i, :], picked_b[:, PACK + i, :], COPY, scale=factor[:, 1, i : i + 1])
+
+        def last_plane(i, cols, list_cols):
             nc.vector.tensor_tensor(
-                u_planes[a][:, i, cols], xa_sb[a][i][:].indirect(list_a[:, list_cols]),
-                scaled_b[:, a * PACK + i, cols], ALU.mult,
+                u_planes[1][:, i, cols], xa_last[i][:].indirect(list_a[:, list_cols]), scaled_b[:, i, cols], ALU.mult
             )
 
         halves = [slice(h * HALF, (h + 1) * HALF) for h in range(2)]
@@ -138,9 +138,15 @@ def tile_list_entryproducts_rival_scattered_pl_kernel(
 
         for i in range(PACK):
             pick_b(0, i)
-            pick_a(0, i, whole, list_whole)
+        for i in range(PACK):
+            first_plane(i)
+        w_d = [deal(f"w_d{a}", w_raw[:, a, :], U32) for a in range(PASSES)]
         ws_d = deal("ws_d", ws_raw[:], U32)
-        ws_sd = deal("ws_sd", raw_scales[:, 2 * R : 3 * R], U8)
+        wb_d = deal("wb_d", wb_raw[:].bitcast(U16), U16)
+        w_sd = [deal(f"w_sd{a}", scales[:, a * R : (a + 1) * R], U8) for a in range(PASSES)]
+        ws_sd = deal("ws_sd", scales[:, 2 * R : 3 * R], U8)
+        wb_sd = deal("wb_sd", scales[:, 3 * R : 4 * R], U8)
+        sx_sc = scales[:, 4 * R :]
         b2_sb = []
         for h in range(2):
             bank = psum.tile([P, PACK, HALF], F32, name=f"b2_bank{h}")
@@ -157,7 +163,6 @@ def tile_list_entryproducts_rival_scattered_pl_kernel(
         u_codes = [[sbuf(f"u_codes{a}_{h}", [P, HALF], U32) for h in range(2)] for a in range(PASSES)]
         u_sc = [[sbuf(f"u_sc{a}_{h}", [P, HALF], U8) for h in range(2)] for a in range(PASSES)]
         a_banks = [psum.tile([P, PACK, HALF], F32, name=f"a_bank{h}") for h in range(2)]
-        w_d, w_sd = [], []
 
         def first_product(a):
             for h in range(2):
@@ -175,20 +180,14 @@ def tile_list_entryproducts_rival_scattered_pl_kernel(
                         start=(a == 0 and t == 0), stop=(a == PASSES - 1 and t == PACK - 1),
                     )
 
-        w_d.append(deal("w_d0", w_raw[0][:], U32))
-        w_sd.append(deal("w_sd0", raw_scales[:, 0:R], U8))
         first_product(0)
-
-        for i in range(PACK - 1):
+        for i in range(PACK):
             pick_b(1, i)
-            pick_a(1, i, whole, list_whole)
-        w_d.append(deal("w_d1", w_raw[1][:], U32))
-        w_sd.append(deal("w_sd1", raw_scales[:, R : 2 * R], U8))
-        wb_d = deal("wb_d", wb_raw[:].bitcast(U16), U16)
-        wb_sd = deal("wb_sd", raw_scales[:, 3 * R : 4 * R], U8)
-        pick_b(1, PACK - 1)
+            scale_b(i)
+        for i in range(PACK - 1):
+            last_plane(i, whole, list_whole)
         for h in range(2):
-            pick_a(1, PACK - 1, halves[h], list_halves[h])
+            last_plane(PACK - 1, halves[h], list_halves[h])
         first_product(1)
 
         hid_bf = [sbuf(f"hid_bf{h}", [P, HALF, PACK], BF16) for h in range(2)]
@@ -208,8 +207,8 @@ def tile_list_entryproducts_rival_scattered_pl_kernel(
                     out=p_banks[h][:, t, :], lhsT=wb_d[:, t, :].bitcast(E2M1), lhsT_scale=wb_sd[:, t, :],
                     rhs=hid_codes[h][:].bitcast(E5M2), rhs_scale=hid_sc[h][:], start=True, stop=True,
                 )
-        nc.scalar.copy(p_sb[:, :, halves[0]], p_banks[0][:])
-        nc.vector.tensor_copy(p_sb[:, :, halves[1]], p_banks[1][:])
+        nc.vector.tensor_copy(p_sb[:, :, halves[0]], p_banks[0][:])
+        nc.scalar.copy(p_sb[:, :, halves[1]], p_banks[1][:])
 
         y = sbuf("y", [P, PACK, C], F32)
         out_rows = out_0.rearrange("(p t) c -> t p c", t=PACK)
@@ -218,31 +217,45 @@ def tile_list_entryproducts_rival_scattered_pl_kernel(
             nc.vector.scalar_tensor_tensor(y[:, t, cols], old_sb[t][:, cols], 0.5, pages[t][:, cols], ALU.mult, ALU.add)
 
         for h in range(2):
-            nc.scalar.activation(pages[0][:].indirect(list_c[:, list_halves[h]]), p_sb[:, 0, halves[h]], COPY)
-        nc.vector.tensor_copy(pages[1][:].indirect(list_c[:]), p_sb[:, 1, :])
-        for t in (2, 3):
+            nc.vector.tensor_copy(pages[0][:].indirect(list_c[:, list_halves[h]]), p_sb[:, 0, halves[h]])
+        for t in range(1, PACK):
             nc.scalar.activation(pages[t][:].indirect(list_c[:]), p_sb[:, t, :], COPY)
         for t in range(PACK - 1):
             add_old(t, slice(0, C))
             nc.sync.dma_start(out=out_rows[t], in_=y[:, t, :])
-        chunks = [slice(c0, c0 + CHUNK) for c0 in range(0, C, CHUNK)]
-        for cols in chunks:
-            add_old(PACK - 1, cols)
+        for c0 in range(0, C, CHUNK):
+            add_old(PACK - 1, slice(c0, c0 + CHUNK))
         nc.sync.dma_start(out=out_rows[PACK - 1], in_=y[:, PACK - 1, :])
 
         y_codes = sbuf("y_codes", [P, C], U32)
         y_sc = sbuf("y_sc", [P, C], U8)
-        y_bf = [sbuf(f"y_bf{n}", [P, CHUNK, PACK], BF16) for n in range(len(chunks))]
         words_out = out_1[0].rearrange("p c t -> p (c t)").bitcast(I32)
-        rounders = [nc.scalar.copy, nc.vector.tensor_copy, nc.vector.tensor_copy, nc.scalar.copy]
-        for n, cols in enumerate(chunks):
-            interleave(rounders[n], y_bf[n][:], y[:, :, cols])
-        for n, cols in enumerate(chunks):
+
+        def round_y(copy, start, stop):
+            rounded = sbuf(f"y_bf{start}", [P, stop - start, PACK], BF16)
+            interleave(copy, rounded[:], y[:, :, start:stop])
+            return rounded
+
+        def quantize_y(rounded, first, start, stop):
             nc.vector.quantize_mx(
-                out=y_codes[:, cols].bitcast(E4M3), scales=y_sc[:, cols],
-                in_=y_bf[n][:].rearrange("p c t -> p (c t)"),
+                out=y_codes[:, start:stop].bitcast(E4M3), scales=y_sc[:, start:stop],
+                in_=rounded[:, start - first : stop - first, :].rearrange("p c t -> p (c t)"),
             )
-            nc.sync.dma_start(out=words_out[:, cols], in_=y_codes[:, cols].bitcast(I32))
+
+        def store_codes(start, stop):
+            nc.sync.dma_start(out=words_out[:, start:stop], in_=y_codes[:, start:stop].bitcast(I32))
+
+        by_scalar = [(0, 256), (256, 512), (512, 640)]
+        from_scalar = [round_y(nc.scalar.copy, start, stop) for start, stop in by_scalar]
+        from_vector = round_y(nc.vector.tensor_copy, 640, C)
+        quantize_y(from_scalar[0], 0, 0, 256)
+        quantize_y(from_vector, 640, 768, C)
+        quantize_y(from_vector, 640, 640, 768)
+        store_codes(640, C)
+        quantize_y(from_scalar[1], 256, 256, 512)
+        store_codes(0, 512)
+        quantize_y(from_scalar[2], 512, 512, 640)
+        store_codes(512, 640)
         for q in range(4):
             queue = nc.sync if q % 2 == 0 else nc.scalar
             queue.dma_start(out=out_2[0, 4 * q : 4 * q + 4, :].bitcast(I32), in_=y_sc[32 * q : 32 * q + 4, :].bitcast(I32))

@@ -23,6 +23,7 @@ PASSES = K // (P * PACK)
 HALF = J // 2
 LIST_COLS = J // 16
 CHUNK = 256
+SCALAR_COLS = 576
 SCALE_COLS = 4 * R + J
 
 
@@ -96,10 +97,11 @@ def tile_list_entryproducts_rival_scattered_pl_kernel(
         nc.sync.dma_start(out=xb_sb[1][:], in_=xb_rows[1])
         nc.sync.dma_start(out=w_raw[:].bitcast(I32), in_=w_words.rearrange("a p n t -> p a (n t)").bitcast(I32))
         load_words(ws_raw, ws_words[0])
-        nc.sync.dma_start(out=wb_raw[:].bitcast(I32), in_=wb_words[0].bitcast(I32))
         for i in range(PACK):
+            if i == 2:
+                load_words(sx_w, sx_words[0])
             nc.sync.dma_start(out=xa_last[i][:], in_=xa_rows[1, i])
-        load_words(sx_w, sx_words[0])
+        nc.sync.dma_start(out=wb_raw[:].bitcast(I32), in_=wb_words[0].bitcast(I32))
         nc.sync.dma_start(list_c[:], offs3)
         old_rows = old.rearrange("(p t) c -> t p c", t=PACK)
         for t in range(PACK):
@@ -142,14 +144,13 @@ def tile_list_entryproducts_rival_scattered_pl_kernel(
             first_plane(i)
         w_d = [deal(f"w_d{a}", w_raw[:, a, :], U32) for a in range(PASSES)]
         ws_d = deal("ws_d", ws_raw[:], U32)
-        wb_d = deal("wb_d", wb_raw[:].bitcast(U16), U16)
         w_sd = [deal(f"w_sd{a}", scales[:, a * R : (a + 1) * R], U8) for a in range(PASSES)]
         ws_sd = deal("ws_sd", scales[:, 2 * R : 3 * R], U8)
         wb_sd = deal("wb_sd", scales[:, 3 * R : 4 * R], U8)
         sx_sc = scales[:, 4 * R :]
         b2_sb = []
         for h in range(2):
-            bank = psum.tile([P, PACK, HALF], F32, name=f"b2_bank{h}")
+            bank = psum.tile([P, PACK, HALF], F32, name=f"b2_bank{h}", tag=f"stage1_{h}")
             for t in range(PACK):
                 nc.tensor.matmul_mx(
                     out=bank[:, t, :], lhsT=ws_d[:, t, :].bitcast(E5M2), lhsT_scale=ws_sd[:, t, :],
@@ -162,11 +163,12 @@ def tile_list_entryproducts_rival_scattered_pl_kernel(
         u_bf = [[sbuf(f"u_bf{a}_{h}", [P, HALF, PACK], BF16) for h in range(2)] for a in range(PASSES)]
         u_codes = [[sbuf(f"u_codes{a}_{h}", [P, HALF], U32) for h in range(2)] for a in range(PASSES)]
         u_sc = [[sbuf(f"u_sc{a}_{h}", [P, HALF], U8) for h in range(2)] for a in range(PASSES)]
-        a_banks = [psum.tile([P, PACK, HALF], F32, name=f"a_bank{h}") for h in range(2)]
+        a_banks = [psum.tile([P, PACK, HALF], F32, name=f"a_bank{h}", tag=f"stage1_{h}") for h in range(2)]
+
+        def round_u(a, h, planes):
+            interleave(nc.vector.tensor_copy, u_bf[a][h][:, :, planes], u_planes[a][:, planes, halves[h]])
 
         def first_product(a):
-            for h in range(2):
-                interleave(nc.vector.tensor_copy, u_bf[a][h][:], u_planes[a][:, :, halves[h]])
             for h in range(2):
                 nc.vector.quantize_mx(
                     out=u_codes[a][h][:].bitcast(E5M2), scales=u_sc[a][h][:],
@@ -180,16 +182,26 @@ def tile_list_entryproducts_rival_scattered_pl_kernel(
                         start=(a == 0 and t == 0), stop=(a == PASSES - 1 and t == PACK - 1),
                     )
 
+        for h in range(2):
+            round_u(0, h, slice(0, PACK))
         first_product(0)
         for i in range(PACK):
             pick_b(1, i)
             scale_b(i)
-        for i in range(PACK - 1):
+        for i in range(2):
             last_plane(i, whole, list_whole)
         for h in range(2):
-            last_plane(PACK - 1, halves[h], list_halves[h])
+            round_u(1, h, slice(0, 2))
+        last_plane(2, whole, list_whole)
+        picked_last = sbuf("picked_last", [P, HALF], F32)
+        nc.scalar.activation(picked_last[:], xa_last[3][:].indirect(list_a[:, list_halves[1]]), COPY)
+        last_plane(3, halves[0], list_halves[0])
+        nc.vector.tensor_tensor(u_planes[1][:, 3, halves[1]], picked_last[:], scaled_b[:, 3, halves[1]], ALU.mult)
+        for h in range(2):
+            round_u(1, h, slice(2, PACK))
         first_product(1)
 
+        wb_d = deal("wb_d", wb_raw[:].bitcast(U16), U16)
         hid_bf = [sbuf(f"hid_bf{h}", [P, HALF, PACK], BF16) for h in range(2)]
         hid_codes = [sbuf(f"hid_codes{h}", [P, HALF], U32) for h in range(2)]
         hid_sc = [sbuf(f"hid_sc{h}", [P, HALF], U8) for h in range(2)]
@@ -231,30 +243,27 @@ def tile_list_entryproducts_rival_scattered_pl_kernel(
         y_sc = sbuf("y_sc", [P, C], U8)
         words_out = out_1[0].rearrange("p c t -> p (c t)").bitcast(I32)
 
-        def round_y(copy, start, stop):
-            rounded = sbuf(f"y_bf{start}", [P, stop - start, PACK], BF16)
-            interleave(copy, rounded[:], y[:, :, start:stop])
-            return rounded
+        y_bf = sbuf("y_bf", [P, C, PACK], BF16)
 
-        def quantize_y(rounded, first, start, stop):
+        def quantize_y(start, stop):
             nc.vector.quantize_mx(
                 out=y_codes[:, start:stop].bitcast(E4M3), scales=y_sc[:, start:stop],
-                in_=rounded[:, start - first : stop - first, :].rearrange("p c t -> p (c t)"),
+                in_=y_bf[:, start:stop, :].rearrange("p c t -> p (c t)"),
             )
 
         def store_codes(start, stop):
             nc.sync.dma_start(out=words_out[:, start:stop], in_=y_codes[:, start:stop].bitcast(I32))
 
-        by_scalar = [(0, 256), (256, 512), (512, 640)]
-        from_scalar = [round_y(nc.scalar.copy, start, stop) for start, stop in by_scalar]
-        from_vector = round_y(nc.vector.tensor_copy, 640, C)
-        quantize_y(from_scalar[0], 0, 0, 256)
-        quantize_y(from_vector, 640, 768, C)
-        quantize_y(from_vector, 640, 640, 768)
+        for start, stop in ((0, 256), (256, 512), (512, SCALAR_COLS)):
+            interleave(nc.scalar.copy, y_bf[:, start:stop, :], y[:, :, start:stop])
+        interleave(nc.vector.tensor_copy, y_bf[:, SCALAR_COLS:, :], y[:, :, SCALAR_COLS:])
+        quantize_y(0, 256)
+        quantize_y(768, C)
+        quantize_y(640, 768)
         store_codes(640, C)
-        quantize_y(from_scalar[1], 256, 256, 512)
+        quantize_y(256, 512)
         store_codes(0, 512)
-        quantize_y(from_scalar[2], 512, 512, 640)
+        quantize_y(512, 640)
         store_codes(512, 640)
         for q in range(4):
             queue = nc.sync if q % 2 == 0 else nc.scalar

from contextlib import ExitStack

import concourse.mybir as mybir

K, T, J, S, R, L, N, C = 1024, 1024, 256, 512, 512, 512, 512, 1024
FLOPS = 2 * J * (K * R + L * R + R * N)

F32 = mybir.dt.float32
BF16 = mybir.dt.bfloat16
I32 = mybir.dt.int32
U32 = mybir.dt.uint32
U16 = mybir.dt.uint16
U8 = mybir.dt.uint8
E5M2 = mybir.dt.float8_e5m2_x4
E4M3 = mybir.dt.float8_e4m3fn_x4
E2M1 = mybir.dt.float4_e2m1fn_x4
ALU = mybir.AluOpType
COPY = mybir.ActivationFunctionType.Copy

P = 128
PACK = 4
PASSES = K // (P * PACK)
HALF = J // 2
LIST_COLS = J // 16
CHUNK = 256
SCALAR_COLS = 576
SCALE_COLS = 4 * R + J


def interleave(copy, dst, src):
    copy(dst.rearrange("p (c i) t -> p c t i", i=4), src.rearrange("p t (c i) -> p c t i", i=4))


def tile_list_entryproducts_rival_scattered_pl_kernel(
    tc, xa, xb, fk, w_words, w_scales, sx_words, sx_scales, ws_words, ws_scales, wb_words, wb_scales,
    old, offs, offs2, offs3, out_0, out_1, out_2,
):
    nc = tc.nc
    with ExitStack() as ctx:
        keep = ctx.enter_context(tc.tile_pool(name="keep", bufs=1))
        psum = ctx.enter_context(tc.psum_pool(name="psum", bufs=1))

        def sbuf(name, shape, dtype):
            return keep.tile(shape, dtype, name=name, align_bytes=64)

        list_a = keep.tile([P, LIST_COLS], U16, name="list_a")
        list_b = keep.tile([P, LIST_COLS], U16, name="list_b")
        list_c = keep.tile([P, LIST_COLS], U16, name="list_c")
        factor = sbuf("factor", [P, PASSES, PACK], F32)

        staged = sbuf("staged", [P, 4, SCALE_COLS // 4], I32)
        scales = sbuf("scales", [P, SCALE_COLS], U8)
        scale_words = scales[:].bitcast(I32)
        nc.vector.memset(scale_words, 0)
        pages = [sbuf(f"page{t}", [P, C], F32) for t in range(PACK)]
        for t in range(PACK):
            nc.vector.memset(pages[t][:], 0.0)

        def load_scales(start, src):
            width = src.shape[1] // 4
            nc.sync.dma_start(
                out=staged[0:P:32, :, start // 4 : start // 4 + width],
                in_=src.bitcast(I32).rearrange("(q r) n -> q r n", r=4),
            )

        def spread_scales(r):
            nc.sync.dma_start(out=scale_words[r:P:32, :], in_=staged[0:P:32, r, :])

        xa_pairs = xa.rearrange("(a p u e) t -> a u p e t", a=PASSES, u=2, e=2)
        xa_rows = xa.rearrange("(a p i) t -> a i p t", a=PASSES, i=PACK)
        xb_rows = xb.rearrange("(a p i) s -> a p i s", a=PASSES, i=PACK)
        xa_first = [sbuf(f"xa0_{u}", [P, 2, T], F32) for u in range(2)]
        xa_last = [sbuf(f"xa1_{i}", [P, T], F32) for i in range(PACK)]
        xb_sb = [sbuf(f"xb{a}", [P, PACK, S], F32) for a in range(PASSES)]
        w_raw = sbuf("w_raw", [P, PASSES, R], U32)
        ws_raw = sbuf("ws_raw", [P, R], U32)
        sx_w = sbuf("sx_w", [P, J], U32)
        wb_raw = sbuf("wb_raw", [P, 2 * N], U8)
        old_sb = [sbuf(f"old{t}", [P, C], F32) for t in range(PACK)]

        def load_words(dst, src):
            nc.sync.dma_start(out=dst[:].bitcast(I32), in_=src.rearrange("p n t -> p (n t)").bitcast(I32))

        nc.sync.dma_start(out=xb_sb[0][:], in_=xb_rows[0])
        load_scales(0, w_scales[0])
        load_scales(R, w_scales[1])
        load_scales(2 * R, ws_scales[0])
        load_scales(3 * R, wb_scales[0])
        load_scales(4 * R, sx_scales[0])
        nc.sync.dma_start(list_b[:], offs2)
        nc.sync.dma_start(out=xa_first[0][:], in_=xa_pairs[0, 0])
        nc.sync.dma_start(list_a[:], offs)
        nc.sync.dma_start(out=factor[:], in_=fk.rearrange("(a p i) o -> p a (i o)", a=PASSES, i=PACK))
        for r in range(4):
            spread_scales(r)
        nc.sync.dma_start(out=xa_first[1][:], in_=xa_pairs[0, 1])
        nc.sync.dma_start(out=xb_sb[1][:], in_=xb_rows[1])
        nc.sync.dma_start(out=w_raw[:].bitcast(I32), in_=w_words.rearrange("a p n t -> p a (n t)").bitcast(I32))
        load_words(ws_raw, ws_words[0])
        for i in range(PACK):
            if i == 2:
                load_words(sx_w, sx_words[0])
            nc.sync.dma_start(out=xa_last[i][:], in_=xa_rows[1, i])
        nc.sync.dma_start(out=wb_raw[:].bitcast(I32), in_=wb_words[0].bitcast(I32))
        nc.sync.dma_start(list_c[:], offs3)
        old_rows = old.rearrange("(p t) c -> t p c", t=PACK)
        for t in range(PACK):
            nc.sync.dma_start(out=old_sb[t][:], in_=old_rows[t])

        def deal(name, raw, dtype):
            dealt = sbuf(name, [P, PACK, P], dtype)
            nc.vector.tensor_copy(dealt[:].rearrange("p t m -> p m t"), raw.rearrange("p (m t) -> p m t", t=PACK))
            return dealt

        picked_b = sbuf("picked_b", [P, PASSES * PACK, J], F32)
        picked_a = sbuf("picked_a", [P, PACK, J], F32)
        scaled_b = sbuf("scaled_b", [P, PACK, J], F32)
        u_planes = [sbuf(f"u_planes{a}", [P, PACK, J], F32) for a in range(PASSES)]

        def pick_b(a, i):
            nc.scalar.activation(picked_b[:, a * PACK + i, :], xb_sb[a][:, i, :].indirect(list_b[:]), COPY)

        def first_plane(i):
            nc.scalar.activation(picked_a[:, i, :], xa_first[i // 2][:, i % 2, :].indirect(list_a[:]), COPY)
            nc.vector.scalar_tensor_tensor(
                u_planes[0][:, i, :], picked_a[:, i, :], factor[:, 0, i : i + 1], picked_b[:, i, :], ALU.mult, ALU.mult
            )

        def scale_b(i):
            nc.scalar.activation(scaled_b[:, i, :], picked_b[:, PACK + i, :], COPY, scale=factor[:, 1, i : i + 1])

        def last_plane(i, cols, list_cols):
            nc.vector.tensor_tensor(
                u_planes[1][:, i, cols], xa_last[i][:].indirect(list_a[:, list_cols]), scaled_b[:, i, cols], ALU.mult
            )

        halves = [slice(h * HALF, (h + 1) * HALF) for h in range(2)]
        list_halves = [slice(h * LIST_COLS // 2, (h + 1) * LIST_COLS // 2) for h in range(2)]
        whole, list_whole = slice(0, J), slice(0, LIST_COLS)

        for i in range(PACK):
            pick_b(0, i)
        for i in range(PACK):
            first_plane(i)
        w_d = [deal(f"w_d{a}", w_raw[:, a, :], U32) for a in range(PASSES)]
        ws_d = deal("ws_d", ws_raw[:], U32)
        w_sd = [deal(f"w_sd{a}", scales[:, a * R : (a + 1) * R], U8) for a in range(PASSES)]
        ws_sd = deal("ws_sd", scales[:, 2 * R : 3 * R], U8)
        wb_sd = deal("wb_sd", scales[:, 3 * R : 4 * R], U8)
        sx_sc = scales[:, 4 * R :]
        b2_sb = []
        for h in range(2):
            bank = psum.tile([P, PACK, HALF], F32, name=f"b2_bank{h}", tag=f"stage1_{h}")
            for t in range(PACK):
                nc.tensor.matmul_mx(
                    out=bank[:, t, :], lhsT=ws_d[:, t, :].bitcast(E5M2), lhsT_scale=ws_sd[:, t, :],
                    rhs=sx_w[:, halves[h]].bitcast(E5M2), rhs_scale=sx_sc[:, halves[h]], start=True, stop=True,
                )
            held = sbuf(f"b2_sb{h}", [P, HALF, PACK], F32)
            nc.scalar.copy(held[:], bank[:].rearrange("p t j -> p j t"))
            b2_sb.append(held)

        u_bf = [[sbuf(f"u_bf{a}_{h}", [P, HALF, PACK], BF16) for h in range(2)] for a in range(PASSES)]
        u_codes = [[sbuf(f"u_codes{a}_{h}", [P, HALF], U32) for h in range(2)] for a in range(PASSES)]
        u_sc = [[sbuf(f"u_sc{a}_{h}", [P, HALF], U8) for h in range(2)] for a in range(PASSES)]
        a_banks = [psum.tile([P, PACK, HALF], F32, name=f"a_bank{h}", tag=f"stage1_{h}") for h in range(2)]

        def round_u(a, h, planes):
            interleave(nc.vector.tensor_copy, u_bf[a][h][:, :, planes], u_planes[a][:, planes, halves[h]])

        def first_product(a):
            for h in range(2):
                nc.vector.quantize_mx(
                    out=u_codes[a][h][:].bitcast(E5M2), scales=u_sc[a][h][:],
                    in_=u_bf[a][h][:].rearrange("p j t -> p (j t)"),
                )
            for h in range(2):
                for t in range(PACK):
                    nc.tensor.matmul_mx(
                        out=a_banks[h][:, t, :], lhsT=w_d[a][:, t, :].bitcast(E5M2), lhsT_scale=w_sd[a][:, t, :],
                        rhs=u_codes[a][h][:].bitcast(E5M2), rhs_scale=u_sc[a][h][:],
                        start=(a == 0 and t == 0), stop=(a == PASSES - 1 and t == PACK - 1),
                    )

        for h in range(2):
            round_u(0, h, slice(0, PACK))
        first_product(0)
        for i in range(PACK):
            pick_b(1, i)
            scale_b(i)
        for i in range(2):
            last_plane(i, whole, list_whole)
        for h in range(2):
            round_u(1, h, slice(0, 2))
        last_plane(2, whole, list_whole)
        picked_last = sbuf("picked_last", [P, HALF], F32)
        nc.scalar.activation(picked_last[:], xa_last[3][:].indirect(list_a[:, list_halves[1]]), COPY)
        last_plane(3, halves[0], list_halves[0])
        nc.vector.tensor_tensor(u_planes[1][:, 3, halves[1]], picked_last[:], scaled_b[:, 3, halves[1]], ALU.mult)
        for h in range(2):
            round_u(1, h, slice(2, PACK))
        first_product(1)

        wb_d = deal("wb_d", wb_raw[:].bitcast(U16), U16)
        hid_bf = [sbuf(f"hid_bf{h}", [P, HALF, PACK], BF16) for h in range(2)]
        hid_codes = [sbuf(f"hid_codes{h}", [P, HALF], U32) for h in range(2)]
        hid_sc = [sbuf(f"hid_sc{h}", [P, HALF], U8) for h in range(2)]
        p_banks = [psum.tile([P, PACK, HALF], F32, name=f"p_bank{h}") for h in range(2)]
        p_sb = sbuf("p_sb", [P, PACK, J], F32)
        for h in range(2):
            nc.vector.tensor_tensor(hid_bf[h][:], a_banks[h][:].rearrange("p t j -> p j t"), b2_sb[h][:], ALU.max)
        for h in range(2):
            nc.vector.quantize_mx(
                out=hid_codes[h][:].bitcast(E5M2), scales=hid_sc[h][:],
                in_=hid_bf[h][:].rearrange("p j t -> p (j t)"),
            )
            for t in range(PACK):
                nc.tensor.matmul_mx(
                    out=p_banks[h][:, t, :], lhsT=wb_d[:, t, :].bitcast(E2M1), lhsT_scale=wb_sd[:, t, :],
                    rhs=hid_codes[h][:].bitcast(E5M2), rhs_scale=hid_sc[h][:], start=True, stop=True,
                )
        nc.vector.tensor_copy(p_sb[:, :, halves[0]], p_banks[0][:])
        nc.scalar.copy(p_sb[:, :, halves[1]], p_banks[1][:])

        y = sbuf("y", [P, PACK, C], F32)
        out_rows = out_0.rearrange("(p t) c -> t p c", t=PACK)

        def add_old(t, cols):
            nc.vector.scalar_tensor_tensor(y[:, t, cols], old_sb[t][:, cols], 0.5, pages[t][:, cols], ALU.mult, ALU.add)

        for h in range(2):
            nc.vector.tensor_copy(pages[0][:].indirect(list_c[:, list_halves[h]]), p_sb[:, 0, halves[h]])
        for t in range(1, PACK):
            nc.scalar.activation(pages[t][:].indirect(list_c[:]), p_sb[:, t, :], COPY)
        for t in range(PACK - 1):
            add_old(t, slice(0, C))
            nc.sync.dma_start(out=out_rows[t], in_=y[:, t, :])
        for c0 in range(0, C, CHUNK):
            add_old(PACK - 1, slice(c0, c0 + CHUNK))
        nc.sync.dma_start(out=out_rows[PACK - 1], in_=y[:, PACK - 1, :])

        y_codes = sbuf("y_codes", [P, C], U32)
        y_sc = sbuf("y_sc", [P, C], U8)
        words_out = out_1[0].rearrange("p c t -> p (c t)").bitcast(I32)

        y_bf = sbuf("y_bf", [P, C, PACK], BF16)

        def quantize_y(start, stop):
            nc.vector.quantize_mx(
                out=y_codes[:, start:stop].bitcast(E4M3), scales=y_sc[:, start:stop],
                in_=y_bf[:, start:stop, :].rearrange("p c t -> p (c t)"),
            )

        def store_codes(start, stop):
            nc.sync.dma_start(out=words_out[:, start:stop], in_=y_codes[:, start:stop].bitcast(I32))

        for start, stop in ((0, 256), (256, 512), (512, SCALAR_COLS)):
            interleave(nc.scalar.copy, y_bf[:, start:stop, :], y[:, :, start:stop])
        interleave(nc.vector.tensor_copy, y_bf[:, SCALAR_COLS:, :], y[:, :, SCALAR_COLS:])
        quantize_y(0, 256)
        quantize_y(768, C)
        quantize_y(640, 768)
        store_codes(640, C)
        quantize_y(256, 512)
        store_codes(0, 512)
        quantize_y(512, 640)
        store_codes(512, 640)
        for q in range(4):
            queue = nc.sync if q % 2 == 0 else nc.scalar
            queue.dma_start(out=out_2[0, 4 * q : 4 * q + 4, :].bitcast(I32), in_=y_sc[32 * q : 32 * q + 4, :].bitcast(I32))
